import numpy as np
import ml_dtypes


def mxq(x, axis, fmt="e4m3"):
    dtype, down = {"e4m3": (ml_dtypes.float8_e4m3fn, 7), "e5m2": (ml_dtypes.float8_e5m2, 14)}[fmt]
    v = np.moveaxis(np.asarray(x, np.float32).astype(ml_dtypes.bfloat16).astype(np.float64), axis, -1)
    blocks = v.reshape(v.shape[:-1] + (-1, 32))
    amax = np.abs(blocks).max(-1, keepdims=True)
    byte = np.maximum(np.where(amax > 0, np.frexp(amax)[1] - 1 + 127, 0) - down, 1)
    scale = np.exp2(byte - 127.0)
    codes = (blocks / scale).astype(np.float32).astype(dtype).astype(np.float64)
    return np.moveaxis((codes * scale).reshape(v.shape), -1, axis)


WIDE = False


def mx_kscale(k):
    if not WIDE:
        return np.ones(k)
    levels = np.array([30, -30])
    if k % 512:
        return np.exp2(np.random.permutation(np.resize(levels, k // 32))).repeat(32)
    a = np.empty((k // 512, 16))
    for p in range(k // 512):
        a[p, :8] = np.random.permutation(np.resize(levels, 8))
        for g in range(8):
            far = levels[np.abs(levels - a[p, g]) >= 10]
            a[p, g + 8] = far[np.random.randint(len(far))]
    return np.exp2(a.ravel()).repeat(32)


def f64(x):
    return np.asarray(x).astype(np.float64)


def striped(idx):
    return np.tile(np.asarray(idx).reshape(-1, 16).T, (8, 1)).astype(np.uint16)


def unstriped(offs):
    return offs[:16].T.reshape(-1).astype(np.int64)


E2M1 = np.array([0.0, 0.5, 1.0, 1.5, 2.0, 3.0, 4.0, 6.0, -0.0, -0.5, -1.0, -1.5, -2.0, -3.0, -4.0, -6.0])


def pack_weight(w, fmt):
    k, n = w.shape
    w = f64(np.asarray(w, np.float32).astype(ml_dtypes.bfloat16)).reshape(k // 32, 32, n)
    amax = np.abs(w).max(1)
    if fmt in ("e4m3", "e5m2"):
        byte = np.frexp(amax)[1] - 1 + 127 - (7 if fmt == "e4m3" else 14)
    else:
        mant, ex = np.frexp(amax / 6.0)
        byte = np.where(mant > 0.5, ex, ex - 1) + 127
    byte = np.clip(np.where(amax > 0, byte, 1), 1, 254)
    scaled = (w * np.exp2(127.0 - byte)[:, None, :]).reshape(k, n).astype(np.float32)
    by_word = np.ascontiguousarray(scaled.reshape(k // 512, 128, 4, n).transpose(0, 1, 3, 2))
    if fmt in ("e4m3", "e5m2"):
        words = by_word.astype(ml_dtypes.float8_e4m3fn if fmt == "e4m3" else ml_dtypes.float8_e5m2).view(np.uint8)
    else:
        c = by_word.astype(ml_dtypes.float4_e2m1fn).view(np.uint8) & 0xF
        words = (c[..., 0::2] | (c[..., 1::2] << 4)).reshape(k // 512, 128, 2 * n)
    return np.ascontiguousarray(words), np.ascontiguousarray(byte.astype(np.uint8).reshape(k // 512, 16, n))


def unpack_weight(words, scales, fmt):
    g, _, n = scales.shape
    words = np.ascontiguousarray(words).reshape(g, 128, n, -1)
    if fmt in ("e4m3", "e5m2"):
        vals = words.view(ml_dtypes.float8_e4m3fn if fmt == "e4m3" else ml_dtypes.float8_e5m2).astype(np.float64)
    else:
        nib = np.empty((g, 128, n, 4), np.uint8)
        nib[..., 0::2] = words & 0xF
        nib[..., 1::2] = words >> 4
        vals = E2M1[nib]
    vals = vals * np.repeat(np.exp2(scales.astype(np.float64) - 127.0), 8, axis=1)[..., None]
    return vals.transpose(0, 1, 3, 2).reshape(g * 512, n)


def bf(x):
    return np.asarray(x, np.float32).astype(ml_dtypes.bfloat16)


def planes(Y):
    r, m = Y.shape
    b = f64(bf(Y)).reshape(r // 32, 32, m)
    amax = np.abs(b).max(1)
    byte = np.clip(np.where(amax > 0, np.frexp(amax)[1] - 1 + 127 - 7, 1), 1, 254)
    codes = (b * np.exp2(127.0 - byte)[:, None, :]).reshape(r, m).astype(np.float32).astype(ml_dtypes.float8_e4m3fn).view(np.uint8)
    words = codes.reshape(r // 512, 128, 4, m).transpose(0, 1, 3, 2)
    return np.ascontiguousarray(words), np.ascontiguousarray(byte.astype(np.uint8).reshape(r // 512, 16, m))


K, T, J, R, L, N = 1024, 1024, 384, 512, 512, 512


def setup_inputs():
    n = np.random.standard_normal
    idx = np.random.permutation(T)[:J]
    fk = mx_kscale(K)
    fr = mx_kscale(R)
    fl = mx_kscale(L)
    wp = pack_weight(n((K, R)) * 1 / np.sqrt(K) * fk[:, None] * fr, "e5m2")
    sxp = pack_weight(n((L, J)) / fl[:, None], "e2m1")
    wsp = pack_weight(n((L, R)) * 1 / np.sqrt(L) * fl[:, None] * fr, "e2m1")
    wbp = pack_weight(n((R, N)) * 1 / np.sqrt(R) / fr[:, None], "e5m2")
    return {
        "xf": (n((K, T))).astype(np.float32),
        "fk": (np.random.uniform(0.5, 2.0, (K, 1)) / fk[:, None]).astype(np.float32),
        "w_words": wp[0],
        "w_scales": wp[1],
        "sx_words": sxp[0],
        "sx_scales": sxp[1],
        "ws_words": wsp[0],
        "ws_scales": wsp[1],
        "wb_words": wbp[0],
        "wb_scales": wbp[1],
        "rs": (n((N, J))).astype(np.float32),
        "gm": (np.random.uniform(0.5, 2.0, (N, 1))).astype(np.float32),
        "offs": striped(idx),
    }


def reference(xf, fk, w_words, w_scales, sx_words, sx_scales, ws_words, ws_scales, wb_words, wb_scales, rs, gm, offs):
    idx = unstriped(offs)
    wu = unpack_weight(w_words, w_scales, "e5m2")
    sxu = unpack_weight(sx_words, sx_scales, "e2m1")
    wsu = unpack_weight(ws_words, ws_scales, "e2m1")
    wbu = unpack_weight(wb_words, wb_scales, "e5m2")
    xg = f64(xf)[:, idx]
    x1 = np.pad(xg, ((0, 0), (1, 0)))[:, :J]
    u = (xg - 0.6 * x1) * f64(fk)
    uq = mxq(u, 0, "e4m3")
    a = wu.T @ uq
    b2 = wsu.T @ sxu
    hid = np.maximum(a, b2)
    hidq = mxq(hid, 0, "e4m3")
    p = wbu.T @ hidq
    y = f64(gm) * p + f64(rs)
    words, scales = planes(y)
    return y, words, scales

@@ -1,0 +1,236 @@
+from contextlib import ExitStack
+
+import concourse.mybir as mybir
+
+K, T, J, R, L, N = 1024, 1024, 384, 512, 512, 512
+FLOPS = 2 * J * (K * R + L * R + R * N)
+
+F32 = mybir.dt.float32
+BF16 = mybir.dt.bfloat16
+I32 = mybir.dt.int32
+U32 = mybir.dt.uint32
+U16 = mybir.dt.uint16
+U8 = mybir.dt.uint8
+E4M3 = mybir.dt.float8_e4m3fn_x4
+E5M2 = mybir.dt.float8_e5m2_x4
+E2M1 = mybir.dt.float4_e2m1fn_x4
+MULT, ADD, MAX = mybir.AluOpType.mult, mybir.AluOpType.add, mybir.AluOpType.max
+COPY = mybir.ActivationFunctionType.Copy
+
+P = 128
+PACK = 4
+PASSES = K // (P * PACK)
+PLANES = PASSES * PACK
+CH = 128
+CHUNKS = J // CH
+LEAD = 8
+STEP = -0.6
+
+
+def tile_list_steps_rival_residual_pl_kernel(
+    tc, xf, fk, w_words, w_scales, sx_words, sx_scales, ws_words, ws_scales, wb_words, wb_scales, rs, gm, offs,
+    out_0, out_1, out_2,
+):
+    nc = tc.nc
+    with ExitStack() as ctx:
+        sb = ctx.enter_context(tc.tile_pool(name="sb", bufs=1))
+        ps = ctx.enter_context(tc.psum_pool(name="ps", bufs=1))
+
+        def tile(name, shape, dtype):
+            return sb.tile(shape, dtype, name=name, align_bytes=64)
+
+        offsets = sb.tile([P, J // 16], U16, name="offsets")
+        x = [tile("x%d" % k, [P, T], F32) for k in range(PLANES)]
+        g_all = tile("g_all", [P, PLANES, LEAD + J], F32)
+        g = [g_all[:, k, :] for k in range(PLANES)]
+        zeros = tile("zeros", [P, PLANES], F32)
+        d = [tile("d%d" % k, [P, J], F32) for k in range(PLANES)]
+        fk_sb = tile("fk_sb", [P, PASSES, PACK], F32)
+        gm_sb = tile("gm_sb", [P, PACK], F32)
+        rs_sb = tile("rs_sb", [P, PACK, J], F32)
+
+        w_raw = tile("w_raw", [P, PASSES, R], U32)
+        w_dealt = tile("w_dealt", [P, PASSES, R], U32)
+        w_sc_raw = tile("w_sc_raw", [P, PASSES, R], U8)
+        w_sc = tile("w_sc", [P, PASSES, R], U8)
+        ws_raw = tile("ws_raw", [P, 2 * R], U8)
+        ws_dealt = tile("ws_dealt", [P, 2 * R], U8)
+        ws_sc_raw = tile("ws_sc_raw", [P, R], U8)
+        ws_sc = tile("ws_sc", [P, R], U8)
+        sx_sb = tile("sx_sb", [P, 2 * J], U8)
+        sx_sc = tile("sx_sc", [P, J], U8)
+        wb_raw = tile("wb_raw", [P, N], U32)
+        wb_dealt = tile("wb_dealt", [P, N], U32)
+        wb_sc_raw = tile("wb_sc_raw", [P, N], U8)
+        wb_sc = tile("wb_sc", [P, N], U8)
+
+        xv = xf.rearrange("(a p t) c -> a t p c", a=PASSES, t=PACK)
+
+        def load_x(k):
+            nc.sync.dma_start(out=x[k][:], in_=xv[k // PACK, k % PACK])
+
+        def load_scales(dst, src):
+            for q in range(4):
+                nc.sync.dma_start(
+                    out=dst[32 * q : 32 * q + 4].bitcast(I32),
+                    in_=src.rearrange("z q c -> q z c")[4 * q : 4 * q + 4].bitcast(I32),
+                )
+
+        def one(t):
+            return t[:].rearrange("p (z c) -> p z c", z=1)
+
+        nc.gpsimd.memset(ws_sc_raw[:].bitcast(I32), 0)
+        nc.vector.memset(zeros[:], 0.0)
+        nc.gpsimd.memset(sx_sc[:].bitcast(I32), 0)
+        nc.vector.memset(w_sc_raw[:].bitcast(I32), 0)
+        nc.vector.memset(wb_sc_raw[:].bitcast(I32), 0)
+        nc.scalar.activation(g_all[:, :, LEAD - 1], zeros[:], COPY)
+
+        nc.sync.dma_start(offsets[:], offs)
+        load_x(0)
+        load_x(1)
+        nc.sync.dma_start(out=fk_sb[:], in_=fk.rearrange("(a p t) o -> p a (t o)", a=PASSES, t=PACK))
+        load_scales(one(ws_sc_raw), ws_scales)
+        nc.sync.dma_start(out=ws_raw[:].bitcast(I32), in_=ws_words[0].bitcast(I32))
+        load_x(2)
+        nc.sync.dma_start(out=sx_sb[:].bitcast(I32), in_=sx_words[0].bitcast(I32))
+        load_scales(one(sx_sc), sx_scales)
+        load_x(3)
+        nc.sync.dma_start(out=w_raw[:].bitcast(I32), in_=w_words.rearrange("z p n t -> p z (n t)").bitcast(I32))
+        load_scales(w_sc_raw[:], w_scales)
+        load_x(4)
+        load_x(5)
+        load_scales(one(wb_sc_raw), wb_scales)
+        load_x(6)
+        load_x(7)
+        nc.sync.dma_start(out=wb_raw[:].bitcast(I32), in_=wb_words[0].rearrange("p n t -> p (n t)").bitcast(I32))
+        nc.sync.dma_start(out=gm_sb[:], in_=gm.rearrange("(p t) o -> p (t o)", t=PACK))
+        nc.sync.dma_start(out=rs_sb[:], in_=rs.rearrange("(p t) j -> p t j", t=PACK))
+
+        u_planes = tile("u_planes", [P, PACK, J], BF16)
+        u_bf = [tile("u_bf%d" % a, [P, J, PACK], BF16) for a in range(PASSES)]
+        u_q = [tile("u_q%d" % a, [P, J], U32) for a in range(PASSES)]
+        u_sc = [tile("u_sc%d" % a, [P, J], U8) for a in range(PASSES)]
+        b2 = tile("b2", [P, J, PACK], F32)
+        a_ps = [ps.tile([P, PACK, CH], F32, name="a_ps%d" % c) for c in range(CHUNKS)]
+
+        def cols(c):
+            return slice(c * CH, (c + 1) * CH)
+
+        def gather(k, j0, j1):
+            nc.scalar.activation(
+                g[k][:, LEAD + j0 : LEAD + j1], x[k][:].indirect(offsets[:, j0 // 16 : j1 // 16]), COPY
+            )
+
+        def steps(k, j0, j1):
+            nc.vector.scalar_tensor_tensor(
+                out=d[k][:, j0:j1], in0=g[k][:, LEAD - 1 + j0 : LEAD - 1 + j1], scalar=STEP,
+                in1=g[k][:, LEAD + j0 : LEAD + j1], op0=MULT, op1=ADD,
+            )
+
+        def factor(k, out, j0, j1):
+            a, t = divmod(k, PACK)
+            nc.vector.tensor_scalar(
+                out=out, in0=d[k][:, j0:j1], scalar1=fk_sb[:, a, t : t + 1], scalar2=None, op0=MULT
+            )
+
+        def quantize(q, sc, src):
+            nc.vector.quantize_mx(out=q.bitcast(E4M3), scales=sc, in_=src.rearrange("p j t -> p (j t)"))
+
+        def deal(engine_copy, dst, src):
+            engine_copy(out=dst.rearrange("p z (t q) -> p z t q", t=PACK), in_=src.rearrange("p z (q t) -> p z t q", t=PACK))
+
+        def first_product(a, c):
+            for t in range(PACK):
+                m = slice(t * P, (t + 1) * P)
+                nc.tensor.matmul_mx(
+                    out=a_ps[c][:, t, :], lhsT=w_dealt[:, a, m].bitcast(E5M2), lhsT_scale=w_sc[:, a, m],
+                    rhs=u_q[a][:, cols(c)].bitcast(E4M3), rhs_scale=u_sc[a][:, cols(c)],
+                    start=(a == 0 and t == 0), stop=(a == PASSES - 1 and t == PACK - 1),
+                )
+
+        for k in range(PACK):
+            gather(k, 0, J)
+            steps(k, 0, J)
+            factor(k, u_planes[:, k, :], 0, J)
+            if k == 1:
+                deal(nc.vector.tensor_copy, one(ws_sc), one(ws_sc_raw))
+                deal(nc.scalar.copy, one(ws_dealt).bitcast(U16), one(ws_raw).bitcast(U16))
+            if k == 2:
+                for c in range(CHUNKS):
+                    b_ps = ps.tile([P, PACK, CH], F32, name="b_ps%d" % c, tag="bank%d" % c)
+                    for t in range(PACK):
+                        nc.tensor.matmul_mx(
+                            out=b_ps[:, t, :], lhsT=ws_dealt[:, 2 * t * P : 2 * (t + 1) * P].bitcast(E2M1),
+                            lhsT_scale=ws_sc[:, t * P : (t + 1) * P],
+                            rhs=sx_sb[:, 2 * c * CH : 2 * (c + 1) * CH].bitcast(E2M1), rhs_scale=sx_sc[:, cols(c)],
+                            start=True, stop=True,
+                        )
+                    nc.scalar.copy(out=b2[:, cols(c), :], in_=b_ps[:].rearrange("p t j -> p j t"))
+        nc.vector.tensor_copy(
+            out=u_bf[0][:].rearrange("p (c i) t -> p c t i", i=4),
+            in_=u_planes[:].rearrange("p t (c i) -> p c t i", i=4),
+        )
+        for a in range(PASSES):
+            deal(nc.scalar.copy, w_dealt[:, a : a + 1, :], w_raw[:, a : a + 1, :])
+        quantize(u_q[0][:], u_sc[0][:], u_bf[0][:])
+        deal(nc.vector.tensor_copy, w_sc[:], w_sc_raw[:])
+        for c in range(CHUNKS):
+            first_product(0, c)
+
+        for k in range(PACK, PLANES - 1):
+            gather(k, 0, J)
+            steps(k, 0, J)
+            factor(k, u_bf[1][:, :, k % PACK], 0, J)
+        deal(nc.vector.tensor_copy, one(wb_sc), one(wb_sc_raw))
+        k = PLANES - 1
+        for c in range(CHUNKS):
+            gather(k, c * CH, (c + 1) * CH)
+            steps(k, c * CH, (c + 1) * CH)
+            factor(k, u_bf[1][:, cols(c), k % PACK], c * CH, (c + 1) * CH)
+            quantize(u_q[1][:, cols(c)], u_sc[1][:, cols(c)], u_bf[1][:, cols(c), :])
+            first_product(1, c)
+        deal(nc.scalar.copy, one(wb_dealt), one(wb_raw))
+
+        hid = [tile("hid%d" % c, [P, CH, PACK], BF16) for c in range(CHUNKS)]
+        h_q = tile("h_q", [P, J], U32)
+        h_sc = tile("h_sc", [P, J], U8)
+        y = [tile("y%d" % c, [P, PACK, CH], F32) for c in range(CHUNKS)]
+        y_bf = [tile("y_bf%d" % c, [P, CH, PACK], BF16) for c in range(CHUNKS)]
+        y_q = tile("y_q", [P, J], U32)
+        y_sc = tile("y_sc", [P, J], U8)
+        p_ps = []
+        for c in range(CHUNKS):
+            nc.vector.tensor_tensor(
+                out=hid[c][:], in0=a_ps[c][:].rearrange("p t j -> p j t"), in1=b2[:, cols(c), :], op=MAX
+            )
+            quantize(h_q[:, cols(c)], h_sc[:, cols(c)], hid[c][:])
+            p_ps.append(ps.tile([P, PACK, CH], F32, name="p_ps%d" % c, tag="bank%d" % c))
+            for t in range(PACK):
+                m = slice(t * P, (t + 1) * P)
+                nc.tensor.matmul_mx(
+                    out=p_ps[c][:, t, :], lhsT=wb_dealt[:, m].bitcast(E5M2), lhsT_scale=wb_sc[:, m],
+                    rhs=h_q[:, cols(c)].bitcast(E4M3), rhs_scale=h_sc[:, cols(c)], start=True, stop=True,
+                )
+
+        out_y = out_0.rearrange("(p t) j -> p t j", t=PACK)
+        out_words = out_1[0].rearrange("p j t -> p (j t)").bitcast(I32)
+        for c in range(CHUNKS):
+            for t in range(PACK):
+                nc.vector.scalar_tensor_tensor(
+                    out=y[c][:, t, :], in0=p_ps[c][:, t, :], scalar=gm_sb[:, t : t + 1], in1=rs_sb[:, t, cols(c)],
+                    op0=MULT, op1=ADD,
+                )
+            nc.sync.dma_start(out=out_y[:, :, cols(c)], in_=y[c][:])
+            weave = nc.scalar.copy if c < CHUNKS - 1 else nc.vector.tensor_copy
+            weave(
+                out=y_bf[c][:].rearrange("p (c i) t -> p c t i", i=4),
+                in_=y[c][:].rearrange("p t (c i) -> p c t i", i=4),
+            )
+            quantize(y_q[:, cols(c)], y_sc[:, cols(c)], y_bf[c][:])
+            nc.sync.dma_start(out=out_words[:, cols(c)], in_=y_q[:, cols(c)].bitcast(I32))
+        for q in range(4):
+            queue = nc.sync if q % 2 else nc.scalar
+            queue.dma_start(
+                out=out_2[0, 4 * q : 4 * q + 4, :].bitcast(I32), in_=y_sc[32 * q : 32 * q + 4, :].bitcast(I32)
+            )

@@ -36,15 +36,16 @@ def tile_list_steps_rival_residual_pl_kernel(
         sb = ctx.enter_context(tc.tile_pool(name="sb", bufs=1))
         ps = ctx.enter_context(tc.psum_pool(name="ps", bufs=1))
 
-        def tile(name, shape, dtype):
-            return sb.tile(shape, dtype, name=name, align_bytes=64)
+        def tile(name, shape, dtype, tag=None):
+            return sb.tile(shape, dtype, name=name, tag=tag or name, align_bytes=64)
 
         offsets = sb.tile([P, J // 16], U16, name="offsets")
         x = [tile("x%d" % k, [P, T], F32) for k in range(PLANES)]
         g_all = tile("g_all", [P, PLANES, LEAD + J], F32)
         g = [g_all[:, k, :] for k in range(PLANES)]
         zeros = tile("zeros", [P, PLANES], F32)
-        d = [tile("d%d" % k, [P, J], F32) for k in range(PLANES)]
+        d_all = tile("d_all", [P, PLANES, J], F32)
+        d = [d_all[:, k, :] for k in range(PLANES)]
         fk_sb = tile("fk_sb", [P, PASSES, PACK], F32)
         gm_sb = tile("gm_sb", [P, PACK], F32)
         rs_sb = tile("rs_sb", [P, PACK, J], F32)
@@ -79,39 +80,37 @@ def tile_list_steps_rival_residual_pl_kernel(
         def one(t):
             return t[:].rearrange("p (z c) -> p z c", z=1)
 
-        nc.gpsimd.memset(ws_sc_raw[:].bitcast(I32), 0)
+        nc.gpsimd.memset(w_sc_raw[:].bitcast(I32), 0)
         nc.vector.memset(zeros[:], 0.0)
+        nc.gpsimd.memset(ws_sc_raw[:].bitcast(I32), 0)
+        nc.gpsimd.memset(wb_sc_raw[:].bitcast(I32), 0)
         nc.gpsimd.memset(sx_sc[:].bitcast(I32), 0)
-        nc.vector.memset(w_sc_raw[:].bitcast(I32), 0)
-        nc.vector.memset(wb_sc_raw[:].bitcast(I32), 0)
         nc.scalar.activation(g_all[:, :, LEAD - 1], zeros[:], COPY)
 
         nc.sync.dma_start(offsets[:], offs)
         load_x(0)
-        load_x(1)
+        load_scales(w_sc_raw[:], w_scales)
         nc.sync.dma_start(out=fk_sb[:], in_=fk.rearrange("(a p t) o -> p a (t o)", a=PASSES, t=PACK))
-        load_scales(one(ws_sc_raw), ws_scales)
-        nc.sync.dma_start(out=ws_raw[:].bitcast(I32), in_=ws_words[0].bitcast(I32))
+        load_x(1)
         load_x(2)
+        load_x(3)
+        load_scales(one(ws_sc_raw), ws_scales)
+        load_x(4)
+        nc.sync.dma_start(out=ws_raw[:].bitcast(I32), in_=ws_words[0].bitcast(I32))
+        nc.sync.dma_start(out=w_raw[:].bitcast(I32), in_=w_words.rearrange("z p n t -> p z (n t)").bitcast(I32))
+        load_scales(one(wb_sc_raw), wb_scales)
+        load_x(5)
+        load_x(6)
         nc.sync.dma_start(out=sx_sb[:].bitcast(I32), in_=sx_words[0].bitcast(I32))
         load_scales(one(sx_sc), sx_scales)
-        load_x(3)
-        nc.sync.dma_start(out=w_raw[:].bitcast(I32), in_=w_words.rearrange("z p n t -> p z (n t)").bitcast(I32))
-        load_scales(w_sc_raw[:], w_scales)
-        load_x(4)
-        load_x(5)
-        load_scales(one(wb_sc_raw), wb_scales)
-        load_x(6)
         load_x(7)
         nc.sync.dma_start(out=wb_raw[:].bitcast(I32), in_=wb_words[0].rearrange("p n t -> p (n t)").bitcast(I32))
         nc.sync.dma_start(out=gm_sb[:], in_=gm.rearrange("(p t) o -> p (t o)", t=PACK))
         nc.sync.dma_start(out=rs_sb[:], in_=rs.rearrange("(p t) j -> p t j", t=PACK))
 
-        u_planes = tile("u_planes", [P, PACK, J], BF16)
         u_bf = [tile("u_bf%d" % a, [P, J, PACK], BF16) for a in range(PASSES)]
         u_q = [tile("u_q%d" % a, [P, J], U32) for a in range(PASSES)]
         u_sc = [tile("u_sc%d" % a, [P, J], U8) for a in range(PASSES)]
-        b2 = tile("b2", [P, J, PACK], F32)
         a_ps = [ps.tile([P, PACK, CH], F32, name="a_ps%d" % c) for c in range(CHUNKS)]
 
         def cols(c):
@@ -134,11 +133,22 @@ def tile_list_steps_rival_residual_pl_kernel(
                 out=out, in0=d[k][:, j0:j1], scalar1=fk_sb[:, a, t : t + 1], scalar2=None, op0=MULT
             )
 
+        def weave_factors(a, planes):
+            nc.vector.tensor_tensor(
+                out=u_bf[a][:, :, 0:planes].rearrange("p (c i) t -> p c t i", i=4),
+                in0=d_all[:, a * PACK : a * PACK + planes, :].rearrange("p t (c i) -> p c t i", i=4),
+                in1=fk_sb[:, a, 0:planes].unsqueeze(1).unsqueeze(3).to_broadcast([P, J // 4, planes, 4]),
+                op=MULT,
+            )
+
         def quantize(q, sc, src):
             nc.vector.quantize_mx(out=q.bitcast(E4M3), scales=sc, in_=src.rearrange("p j t -> p (j t)"))
 
         def deal(engine_copy, dst, src):
-            engine_copy(out=dst.rearrange("p z (t q) -> p z t q", t=PACK), in_=src.rearrange("p z (q t) -> p z t q", t=PACK))
+            engine_copy(
+                out=dst.rearrange("p z (t c i) -> p z c t i", t=PACK, i=4),
+                in_=src.rearrange("p z (c i t) -> p z c t i", t=PACK, i=4),
+            )
 
         def first_product(a, c):
             for t in range(PACK):
@@ -149,43 +159,43 @@ def tile_list_steps_rival_residual_pl_kernel(
                     start=(a == 0 and t == 0), stop=(a == PASSES - 1 and t == PACK - 1),
                 )
 
+        def rival_product(c):
+            b_ps = ps.tile([P, PACK, CH], F32, name="b_ps%d" % c, tag="bank%d" % c)
+            for t in range(PACK):
+                nc.tensor.matmul_mx(
+                    out=b_ps[:, t, :], lhsT=ws_dealt[:, 2 * t * P : 2 * (t + 1) * P].bitcast(E2M1),
+                    lhsT_scale=ws_sc[:, t * P : (t + 1) * P],
+                    rhs=sx_sb[:, 2 * c * CH : 2 * (c + 1) * CH].bitcast(E2M1), rhs_scale=sx_sc[:, cols(c)],
+                    start=True, stop=True,
+                )
+            return b_ps
+
+        deal(nc.vector.tensor_copy, w_sc[:], w_sc_raw[:])
         for k in range(PACK):
             gather(k, 0, J)
             steps(k, 0, J)
-            factor(k, u_planes[:, k, :], 0, J)
-            if k == 1:
-                deal(nc.vector.tensor_copy, one(ws_sc), one(ws_sc_raw))
-                deal(nc.scalar.copy, one(ws_dealt).bitcast(U16), one(ws_raw).bitcast(U16))
-            if k == 2:
-                for c in range(CHUNKS):
-                    b_ps = ps.tile([P, PACK, CH], F32, name="b_ps%d" % c, tag="bank%d" % c)
-                    for t in range(PACK):
-                        nc.tensor.matmul_mx(
-                            out=b_ps[:, t, :], lhsT=ws_dealt[:, 2 * t * P : 2 * (t + 1) * P].bitcast(E2M1),
-                            lhsT_scale=ws_sc[:, t * P : (t + 1) * P],
-                            rhs=sx_sb[:, 2 * c * CH : 2 * (c + 1) * CH].bitcast(E2M1), rhs_scale=sx_sc[:, cols(c)],
-                            start=True, stop=True,
-                        )
-                    nc.scalar.copy(out=b2[:, cols(c), :], in_=b_ps[:].rearrange("p t j -> p j t"))
-        nc.vector.tensor_copy(
-            out=u_bf[0][:].rearrange("p (c i) t -> p c t i", i=4),
-            in_=u_planes[:].rearrange("p t (c i) -> p c t i", i=4),
-        )
-        for a in range(PASSES):
-            deal(nc.scalar.copy, w_dealt[:, a : a + 1, :], w_raw[:, a : a + 1, :])
+        weave_factors(0, PACK)
+        deal(nc.vector.tensor_copy, one(ws_sc), one(ws_sc_raw))
         quantize(u_q[0][:], u_sc[0][:], u_bf[0][:])
-        deal(nc.vector.tensor_copy, w_sc[:], w_sc_raw[:])
-        for c in range(CHUNKS):
-            first_product(0, c)
 
         for k in range(PACK, PLANES - 1):
             gather(k, 0, J)
             steps(k, 0, J)
-            factor(k, u_bf[1][:, :, k % PACK], 0, J)
-        deal(nc.vector.tensor_copy, one(wb_sc), one(wb_sc_raw))
+            if k == PACK:
+                deal(nc.scalar.copy, one(ws_dealt).bitcast(U16), one(ws_raw).bitcast(U16))
+                for a in range(PASSES):
+                    deal(nc.scalar.copy, w_dealt[:, a : a + 1, :], w_raw[:, a : a + 1, :])
+                deal(nc.vector.tensor_copy, one(wb_sc), one(wb_sc_raw))
+                for c in range(CHUNKS):
+                    first_product(0, c)
+        weave_factors(1, PACK - 1)
         k = PLANES - 1
         for c in range(CHUNKS):
             gather(k, c * CH, (c + 1) * CH)
+        b2 = tile("b2", [P, CHUNKS, CH // 4, PACK, 4], F32, tag="x%d" % k)
+        for c in range(CHUNKS):
+            nc.scalar.copy(out=b2[:, c], in_=rival_product(c)[:].rearrange("p t (c i) -> p c t i", i=4))
+        for c in range(CHUNKS):
             steps(k, c * CH, (c + 1) * CH)
             factor(k, u_bf[1][:, cols(c), k % PACK], c * CH, (c + 1) * CH)
             quantize(u_q[1][:, cols(c)], u_sc[1][:, cols(c)], u_bf[1][:, cols(c), :])
@@ -202,7 +212,8 @@ def tile_list_steps_rival_residual_pl_kernel(
         p_ps = []
         for c in range(CHUNKS):
             nc.vector.tensor_tensor(
-                out=hid[c][:], in0=a_ps[c][:].rearrange("p t j -> p j t"), in1=b2[:, cols(c), :], op=MAX
+                out=hid[c][:].rearrange("p (c i) t -> p c t i", i=4),
+                in0=a_ps[c][:].rearrange("p t (c i) -> p c t i", i=4), in1=b2[:, c], op=MAX,
             )
             quantize(h_q[:, cols(c)], h_sc[:, cols(c)], hid[c][:])
             p_ps.append(ps.tile([P, PACK, CH], F32, name="p_ps%d" % c, tag="bank%d" % c))

@@ -108,6 +108,7 @@ def tile_list_steps_rival_residual_pl_kernel(
         nc.sync.dma_start(out=gm_sb[:], in_=gm.rearrange("(p t) o -> p (t o)", t=PACK))
         nc.sync.dma_start(out=rs_sb[:], in_=rs.rearrange("(p t) j -> p t j", t=PACK))
 
+        u_planes = tile("u_planes", [P, PLANES - 1, J], BF16)
         u_bf = [tile("u_bf%d" % a, [P, J, PACK], BF16) for a in range(PASSES)]
         u_q = [tile("u_q%d" % a, [P, J], U32) for a in range(PASSES)]
         u_sc = [tile("u_sc%d" % a, [P, J], U8) for a in range(PASSES)]
@@ -133,21 +134,13 @@ def tile_list_steps_rival_residual_pl_kernel(
                 out=out, in0=d[k][:, j0:j1], scalar1=fk_sb[:, a, t : t + 1], scalar2=None, op0=MULT
             )
 
-        def weave_factors(a, planes):
-            nc.vector.tensor_tensor(
-                out=u_bf[a][:, :, 0:planes].rearrange("p (c i) t -> p c t i", i=4),
-                in0=d_all[:, a * PACK : a * PACK + planes, :].rearrange("p t (c i) -> p c t i", i=4),
-                in1=fk_sb[:, a, 0:planes].unsqueeze(1).unsqueeze(3).to_broadcast([P, J // 4, planes, 4]),
-                op=MULT,
-            )
-
         def quantize(q, sc, src):
             nc.vector.quantize_mx(out=q.bitcast(E4M3), scales=sc, in_=src.rearrange("p j t -> p (j t)"))
 
-        def deal(engine_copy, dst, src):
+        def deal(engine_copy, dst, src, run):
             engine_copy(
-                out=dst.rearrange("p z (t c i) -> p z c t i", t=PACK, i=4),
-                in_=src.rearrange("p z (c i t) -> p z c t i", t=PACK, i=4),
+                out=dst.rearrange("p z (t c i) -> p z c t i", t=PACK, i=run),
+                in_=src.rearrange("p z (c i t) -> p z c t i", t=PACK, i=run),
             )
 
         def first_product(a, c):
@@ -170,37 +163,44 @@ def tile_list_steps_rival_residual_pl_kernel(
                 )
             return b_ps
 
-        deal(nc.vector.tensor_copy, w_sc[:], w_sc_raw[:])
+        deal(nc.vector.tensor_copy, w_sc[:], w_sc_raw[:], 16)
         for k in range(PACK):
             gather(k, 0, J)
             steps(k, 0, J)
-        weave_factors(0, PACK)
-        deal(nc.vector.tensor_copy, one(ws_sc), one(ws_sc_raw))
+            factor(k, u_planes[:, k, :], 0, J)
+        nc.vector.tensor_copy(
+            out=u_bf[0][:].rearrange("p (c i) t -> p c t i", i=4),
+            in_=u_planes[:, 0:PACK, :].rearrange("p t (c i) -> p c t i", i=4),
+        )
+        deal(nc.vector.tensor_copy, one(ws_sc), one(ws_sc_raw), 16)
         quantize(u_q[0][:], u_sc[0][:], u_bf[0][:])
 
         for k in range(PACK, PLANES - 1):
             gather(k, 0, J)
             steps(k, 0, J)
+            factor(k, u_planes[:, k, :], 0, J)
             if k == PACK:
-                deal(nc.scalar.copy, one(ws_dealt).bitcast(U16), one(ws_raw).bitcast(U16))
+                deal(nc.scalar.copy, one(ws_dealt).bitcast(U16), one(ws_raw).bitcast(U16), 8)
                 for a in range(PASSES):
-                    deal(nc.scalar.copy, w_dealt[:, a : a + 1, :], w_raw[:, a : a + 1, :])
-                deal(nc.vector.tensor_copy, one(wb_sc), one(wb_sc_raw))
+                    deal(nc.scalar.copy, w_dealt[:, a : a + 1, :], w_raw[:, a : a + 1, :], 4)
+                deal(nc.vector.tensor_copy, one(wb_sc), one(wb_sc_raw), 16)
                 for c in range(CHUNKS):
                     first_product(0, c)
-        weave_factors(1, PACK - 1)
+        nc.vector.tensor_copy(
+            out=u_bf[1][:, :, 0 : PACK - 1], in_=u_planes[:, PACK:, :].rearrange("p t j -> p j t")
+        )
         k = PLANES - 1
         for c in range(CHUNKS):
             gather(k, c * CH, (c + 1) * CH)
-        b2 = tile("b2", [P, CHUNKS, CH // 4, PACK, 4], F32, tag="x%d" % k)
+        b2 = tile("b2", [P, CHUNKS, CH, PACK], F32, tag="x%d" % k)
         for c in range(CHUNKS):
-            nc.scalar.copy(out=b2[:, c], in_=rival_product(c)[:].rearrange("p t (c i) -> p c t i", i=4))
+            nc.scalar.copy(out=b2[:, c], in_=rival_product(c)[:].rearrange("p t j -> p j t"))
         for c in range(CHUNKS):
             steps(k, c * CH, (c + 1) * CH)
             factor(k, u_bf[1][:, cols(c), k % PACK], c * CH, (c + 1) * CH)
             quantize(u_q[1][:, cols(c)], u_sc[1][:, cols(c)], u_bf[1][:, cols(c), :])
             first_product(1, c)
-        deal(nc.scalar.copy, one(wb_dealt), one(wb_raw))
+        deal(nc.scalar.copy, one(wb_dealt), one(wb_raw), 4)
 
         hid = [tile("hid%d" % c, [P, CH, PACK], BF16) for c in range(CHUNKS)]
         h_q = tile("h_q", [P, J], U32)
@@ -212,8 +212,7 @@ def tile_list_steps_rival_residual_pl_kernel(
         p_ps = []
         for c in range(CHUNKS):
             nc.vector.tensor_tensor(
-                out=hid[c][:].rearrange("p (c i) t -> p c t i", i=4),
-                in0=a_ps[c][:].rearrange("p t (c i) -> p c t i", i=4), in1=b2[:, c], op=MAX,
+                out=hid[c][:], in0=a_ps[c][:].rearrange("p t j -> p j t"), in1=b2[:, c], op=MAX
             )
             quantize(h_q[:, cols(c)], h_sc[:, cols(c)], hid[c][:])
             p_ps.append(ps.tile([P, PACK, CH], F32, name="p_ps%d" % c, tag="bank%d" % c))

@@ -50,7 +50,7 @@ def tile_list_steps_rival_residual_pl_kernel(
         gm_sb = tile("gm_sb", [P, PACK], F32)
         rs_sb = tile("rs_sb", [P, PACK, J], F32)
 
-        w_raw = tile("w_raw", [P, PASSES, R], U32)
+        w_raw = [tile("w_raw%d" % a, [P, R], U32) for a in range(PASSES)]
         w_dealt = tile("w_dealt", [P, PASSES, R], U32)
         w_sc_raw = tile("w_sc_raw", [P, PASSES, R], U8)
         w_sc = tile("w_sc", [P, PASSES, R], U8)
@@ -70,8 +70,11 @@ def tile_list_steps_rival_residual_pl_kernel(
         def load_x(k):
             nc.sync.dma_start(out=x[k][:], in_=xv[k // PACK, k % PACK])
 
-        def load_scales(dst, src):
-            for q in range(4):
+        def load_words(dst, src):
+            nc.sync.dma_start(out=dst[:].bitcast(I32), in_=src.rearrange("p n t -> p (n t)").bitcast(I32))
+
+        def load_scales(dst, src, quadrants=range(4)):
+            for q in quadrants:
                 nc.sync.dma_start(
                     out=dst[32 * q : 32 * q + 4].bitcast(I32),
                     in_=src.rearrange("z q c -> q z c")[4 * q : 4 * q + 4].bitcast(I32),
@@ -96,19 +99,21 @@ def tile_list_steps_rival_residual_pl_kernel(
         load_x(3)
         load_scales(one(ws_sc_raw), ws_scales)
         load_x(4)
-        nc.sync.dma_start(out=ws_raw[:].bitcast(I32), in_=ws_words[0].bitcast(I32))
-        nc.sync.dma_start(out=w_raw[:].bitcast(I32), in_=w_words.rearrange("z p n t -> p z (n t)").bitcast(I32))
+        load_words(w_raw[0], w_words[0])
         load_scales(one(wb_sc_raw), wb_scales)
+        load_scales(one(sx_sc), sx_scales, range(0, 1))
         load_x(5)
         load_x(6)
+        load_scales(one(sx_sc), sx_scales, range(1, 4))
+        nc.sync.dma_start(out=ws_raw[:].bitcast(I32), in_=ws_words[0].bitcast(I32))
         nc.sync.dma_start(out=sx_sb[:].bitcast(I32), in_=sx_words[0].bitcast(I32))
-        load_scales(one(sx_sc), sx_scales)
         load_x(7)
-        nc.sync.dma_start(out=wb_raw[:].bitcast(I32), in_=wb_words[0].rearrange("p n t -> p (n t)").bitcast(I32))
+        load_words(w_raw[1], w_words[1])
+        load_words(wb_raw, wb_words[0])
         nc.sync.dma_start(out=gm_sb[:], in_=gm.rearrange("(p t) o -> p (t o)", t=PACK))
         nc.sync.dma_start(out=rs_sb[:], in_=rs.rearrange("(p t) j -> p t j", t=PACK))
 
-        u_planes = tile("u_planes", [P, PLANES - 1, J], BF16)
+        u_planes = tile("u_planes", [P, PLANES, J], BF16)
         u_bf = [tile("u_bf%d" % a, [P, J, PACK], BF16) for a in range(PASSES)]
         u_q = [tile("u_q%d" % a, [P, J], U32) for a in range(PASSES)]
         u_sc = [tile("u_sc%d" % a, [P, J], U8) for a in range(PASSES)]
@@ -180,24 +185,25 @@ def tile_list_steps_rival_residual_pl_kernel(
             steps(k, 0, J)
             factor(k, u_planes[:, k, :], 0, J)
             if k == PACK:
-                deal(nc.scalar.copy, one(ws_dealt).bitcast(U16), one(ws_raw).bitcast(U16), 8)
-                for a in range(PASSES):
-                    deal(nc.scalar.copy, w_dealt[:, a : a + 1, :], w_raw[:, a : a + 1, :], 4)
+                deal(nc.scalar.copy, w_dealt[:, 0:1, :], one(w_raw[0]), 4)
                 deal(nc.vector.tensor_copy, one(wb_sc), one(wb_sc_raw), 16)
                 for c in range(CHUNKS):
                     first_product(0, c)
-        nc.vector.tensor_copy(
-            out=u_bf[1][:, :, 0 : PACK - 1], in_=u_planes[:, PACK:, :].rearrange("p t j -> p j t")
-        )
+        deal(nc.scalar.copy, one(ws_dealt).bitcast(U16), one(ws_raw).bitcast(U16), 8)
         k = PLANES - 1
         for c in range(CHUNKS):
             gather(k, c * CH, (c + 1) * CH)
-        b2 = tile("b2", [P, CHUNKS, CH, PACK], F32, tag="x%d" % k)
+        deal(nc.scalar.copy, w_dealt[:, 1:2, :], one(w_raw[1]), 4)
+        b2 = tile("b2", [P, CHUNKS, CH, PACK], F32, tag="w_raw1")
         for c in range(CHUNKS):
             nc.scalar.copy(out=b2[:, c], in_=rival_product(c)[:].rearrange("p t j -> p j t"))
         for c in range(CHUNKS):
             steps(k, c * CH, (c + 1) * CH)
-            factor(k, u_bf[1][:, cols(c), k % PACK], c * CH, (c + 1) * CH)
+            factor(k, u_planes[:, k, cols(c)], c * CH, (c + 1) * CH)
+            nc.vector.tensor_copy(
+                out=u_bf[1][:, cols(c), :].rearrange("p (c i) t -> p c t i", i=4),
+                in_=u_planes[:, PACK:, cols(c)].rearrange("p t (c i) -> p c t i", i=4),
+            )
             quantize(u_q[1][:, cols(c)], u_sc[1][:, cols(c)], u_bf[1][:, cols(c), :])
             first_product(1, c)
         deal(nc.scalar.copy, one(wb_dealt), one(wb_raw), 4)

@@ -21,10 +21,16 @@ P = 128
 PACK = 4
 PASSES = K // (P * PACK)
 PLANES = PASSES * PACK
+LAST = PLANES - 1
+QUADRANT = 32
+SCALE_ROWS = 4
+LIST_COLUMN = 16
 CH = 128
 CHUNKS = J // CH
 LEAD = 8
 STEP = -0.6
+LINE = 16
+RUN = 4
 
 
 def tile_list_steps_rival_residual_pl_kernel(
@@ -39,7 +45,7 @@ def tile_list_steps_rival_residual_pl_kernel(
         def tile(name, shape, dtype, tag=None):
             return sb.tile(shape, dtype, name=name, tag=tag or name, align_bytes=64)
 
-        offsets = sb.tile([P, J // 16], U16, name="offsets")
+        offsets = sb.tile([P, J // LIST_COLUMN], U16, name="offsets")
         x = [tile("x%d" % k, [P, T], F32) for k in range(PLANES)]
         g_all = tile("g_all", [P, PLANES, LEAD + J], F32)
         g = [g_all[:, k, :] for k in range(PLANES)]
@@ -65,19 +71,19 @@ def tile_list_steps_rival_residual_pl_kernel(
         wb_sc_raw = tile("wb_sc_raw", [P, N], U8)
         wb_sc = tile("wb_sc", [P, N], U8)
 
-        xv = xf.rearrange("(a p t) c -> a t p c", a=PASSES, t=PACK)
+        x_planes = xf.rearrange("(a p t) c -> a t p c", a=PASSES, t=PACK)
 
         def load_x(k):
-            nc.sync.dma_start(out=x[k][:], in_=xv[k // PACK, k % PACK])
+            nc.sync.dma_start(out=x[k][:], in_=x_planes[k // PACK, k % PACK])
 
         def load_words(dst, src):
             nc.sync.dma_start(out=dst[:].bitcast(I32), in_=src.rearrange("p n t -> p (n t)").bitcast(I32))
 
-        def load_scales(dst, src, quadrants=range(4)):
-            for q in quadrants:
+        def load_scales(dst, src, rows=range(SCALE_ROWS)):
+            for r in rows:
                 nc.sync.dma_start(
-                    out=dst[32 * q : 32 * q + 4].bitcast(I32),
-                    in_=src.rearrange("z q c -> q z c")[4 * q : 4 * q + 4].bitcast(I32),
+                    out=dst[r:P:QUADRANT].bitcast(I32),
+                    in_=src.rearrange("z (s r) c -> r s z c", r=SCALE_ROWS)[r].bitcast(I32),
                 )
 
         def one(t):
@@ -90,10 +96,10 @@ def tile_list_steps_rival_residual_pl_kernel(
         nc.gpsimd.memset(sx_sc[:].bitcast(I32), 0)
         nc.scalar.activation(g_all[:, :, LEAD - 1], zeros[:], COPY)
 
-        nc.sync.dma_start(offsets[:], offs)
+        nc.sync.dma_start(out=fk_sb[:], in_=fk.rearrange("(a p t) o -> p a (t o)", a=PASSES, t=PACK))
         load_x(0)
         load_scales(w_sc_raw[:], w_scales)
-        nc.sync.dma_start(out=fk_sb[:], in_=fk.rearrange("(a p t) o -> p a (t o)", a=PASSES, t=PACK))
+        nc.sync.dma_start(offsets[:], offs)
         load_x(1)
         load_x(2)
         load_x(3)
@@ -104,10 +110,10 @@ def tile_list_steps_rival_residual_pl_kernel(
         load_scales(one(sx_sc), sx_scales, range(0, 1))
         load_x(5)
         load_x(6)
-        load_scales(one(sx_sc), sx_scales, range(1, 4))
+        load_scales(one(sx_sc), sx_scales, range(1, SCALE_ROWS))
         nc.sync.dma_start(out=ws_raw[:].bitcast(I32), in_=ws_words[0].bitcast(I32))
         nc.sync.dma_start(out=sx_sb[:].bitcast(I32), in_=sx_words[0].bitcast(I32))
-        load_x(7)
+        load_x(LAST)
         load_words(w_raw[1], w_words[1])
         load_words(wb_raw, wb_words[0])
         nc.sync.dma_start(out=gm_sb[:], in_=gm.rearrange("(p t) o -> p (t o)", t=PACK))
@@ -124,25 +130,36 @@ def tile_list_steps_rival_residual_pl_kernel(
 
         def gather(k, j0, j1):
             nc.scalar.activation(
-                g[k][:, LEAD + j0 : LEAD + j1], x[k][:].indirect(offsets[:, j0 // 16 : j1 // 16]), COPY
+                g[k][:, LEAD + j0 : LEAD + j1],
+                x[k][:].indirect(offsets[:, j0 // LIST_COLUMN : j1 // LIST_COLUMN]),
+                COPY,
             )
 
-        def steps(k, j0, j1):
+        def steps(out, src, j0, j1):
             nc.vector.scalar_tensor_tensor(
-                out=d[k][:, j0:j1], in0=g[k][:, LEAD - 1 + j0 : LEAD - 1 + j1], scalar=STEP,
-                in1=g[k][:, LEAD + j0 : LEAD + j1], op0=MULT, op1=ADD,
+                out=out[:, j0:j1], in0=src[:, LEAD - 1 + j0 : LEAD - 1 + j1], scalar=STEP,
+                in1=src[:, LEAD + j0 : LEAD + j1], op0=MULT, op1=ADD,
             )
 
-        def factor(k, out, j0, j1):
-            a, t = divmod(k, PACK)
+        def fk_of(k):
+            return fk_sb[:, k // PACK, k % PACK : k % PACK + 1]
+
+        def make_u(k, j0, j1):
+            steps(d[k], g[k], j0, j1)
             nc.vector.tensor_scalar(
-                out=out, in0=d[k][:, j0:j1], scalar1=fk_sb[:, a, t : t + 1], scalar2=None, op0=MULT
+                out=u_planes[:, k, j0:j1], in0=d[k][:, j0:j1], scalar1=fk_of(k), scalar2=None, op0=MULT
+            )
+
+        def weave(engine_copy, dst, src):
+            engine_copy(
+                out=dst.rearrange("p (c i) t -> p c t i", i=RUN), in_=src.rearrange("p t (c i) -> p c t i", i=RUN)
             )
 
         def quantize(q, sc, src):
             nc.vector.quantize_mx(out=q.bitcast(E4M3), scales=sc, in_=src.rearrange("p j t -> p (j t)"))
 
-        def deal(engine_copy, dst, src, run):
+        def deal(engine_copy, dst, src, item_bytes):
+            run = LINE // item_bytes
             engine_copy(
                 out=dst.rearrange("p z (t c i) -> p z c t i", t=PACK, i=run),
                 in_=src.rearrange("p z (c i t) -> p z c t i", t=PACK, i=run),
@@ -168,42 +185,34 @@ def tile_list_steps_rival_residual_pl_kernel(
                 )
             return b_ps
 
-        deal(nc.vector.tensor_copy, w_sc[:], w_sc_raw[:], 16)
+        deal(nc.vector.tensor_copy, w_sc[:], w_sc_raw[:], 1)
         for k in range(PACK):
             gather(k, 0, J)
-            steps(k, 0, J)
-            factor(k, u_planes[:, k, :], 0, J)
-        nc.vector.tensor_copy(
-            out=u_bf[0][:].rearrange("p (c i) t -> p c t i", i=4),
-            in_=u_planes[:, 0:PACK, :].rearrange("p t (c i) -> p c t i", i=4),
-        )
-        deal(nc.vector.tensor_copy, one(ws_sc), one(ws_sc_raw), 16)
+            make_u(k, 0, J)
+        weave(nc.vector.tensor_copy, u_bf[0][:], u_planes[:, 0:PACK, :])
+        deal(nc.vector.tensor_copy, one(ws_sc), one(ws_sc_raw), 1)
         quantize(u_q[0][:], u_sc[0][:], u_bf[0][:])
 
-        for k in range(PACK, PLANES - 1):
-            gather(k, 0, J)
-            steps(k, 0, J)
-            factor(k, u_planes[:, k, :], 0, J)
-            if k == PACK:
-                deal(nc.scalar.copy, w_dealt[:, 0:1, :], one(w_raw[0]), 4)
-                deal(nc.vector.tensor_copy, one(wb_sc), one(wb_sc_raw), 16)
-                for c in range(CHUNKS):
-                    first_product(0, c)
-        deal(nc.scalar.copy, one(ws_dealt).bitcast(U16), one(ws_raw).bitcast(U16), 8)
-        k = PLANES - 1
+        gather(PACK, 0, J)
+        make_u(PACK, 0, J)
+        deal(nc.scalar.copy, w_dealt[:, 0:1, :], one(w_raw[0]), 4)
+        deal(nc.vector.tensor_copy, one(wb_sc), one(wb_sc_raw), 1)
         for c in range(CHUNKS):
-            gather(k, c * CH, (c + 1) * CH)
+            first_product(0, c)
+        for k in range(PACK + 1, LAST):
+            gather(k, 0, J)
+            make_u(k, 0, J)
+        deal(nc.scalar.copy, one(ws_dealt).bitcast(U16), one(ws_raw).bitcast(U16), 2)
+
+        for c in range(CHUNKS):
+            gather(LAST, c * CH, (c + 1) * CH)
         deal(nc.scalar.copy, w_dealt[:, 1:2, :], one(w_raw[1]), 4)
         b2 = tile("b2", [P, CHUNKS, CH, PACK], F32, tag="w_raw1")
         for c in range(CHUNKS):
             nc.scalar.copy(out=b2[:, c], in_=rival_product(c)[:].rearrange("p t j -> p j t"))
         for c in range(CHUNKS):
-            steps(k, c * CH, (c + 1) * CH)
-            factor(k, u_planes[:, k, cols(c)], c * CH, (c + 1) * CH)
-            nc.vector.tensor_copy(
-                out=u_bf[1][:, cols(c), :].rearrange("p (c i) t -> p c t i", i=4),
-                in_=u_planes[:, PACK:, cols(c)].rearrange("p t (c i) -> p c t i", i=4),
-            )
+            make_u(LAST, c * CH, (c + 1) * CH)
+            weave(nc.vector.tensor_copy, u_bf[1][:, cols(c), :], u_planes[:, PACK:, cols(c)])
             quantize(u_q[1][:, cols(c)], u_sc[1][:, cols(c)], u_bf[1][:, cols(c), :])
             first_product(1, c)
         deal(nc.scalar.copy, one(wb_dealt), one(wb_raw), 4)
@@ -238,15 +247,15 @@ def tile_list_steps_rival_residual_pl_kernel(
                     op0=MULT, op1=ADD,
                 )
             nc.sync.dma_start(out=out_y[:, :, cols(c)], in_=y[c][:])
-            weave = nc.scalar.copy if c < CHUNKS - 1 else nc.vector.tensor_copy
-            weave(
-                out=y_bf[c][:].rearrange("p (c i) t -> p c t i", i=4),
-                in_=y[c][:].rearrange("p t (c i) -> p c t i", i=4),
-            )
+            weave(nc.scalar.copy if c < CHUNKS - 1 else nc.vector.tensor_copy, y_bf[c][:], y[c][:])
+        for c in range(CHUNKS):
             quantize(y_q[:, cols(c)], y_sc[:, cols(c)], y_bf[c][:])
-            nc.sync.dma_start(out=out_words[:, cols(c)], in_=y_q[:, cols(c)].bitcast(I32))
-        for q in range(4):
-            queue = nc.sync if q % 2 else nc.scalar
+        early = (CHUNKS - 1) * CH
+        nc.sync.dma_start(out=out_words[:, :early], in_=y_q[:, :early].bitcast(I32))
+        nc.sync.dma_start(out=out_words[:, early:], in_=y_q[:, early:].bitcast(I32))
+        for r in range(SCALE_ROWS):
+            queue = nc.sync if r % 2 else nc.scalar
             queue.dma_start(
-                out=out_2[0, 4 * q : 4 * q + 4, :].bitcast(I32), in_=y_sc[32 * q : 32 * q + 4, :].bitcast(I32)
+                out=out_2[0].rearrange("(s r) c -> r s c", r=SCALE_ROWS)[r].bitcast(I32),
+                in_=y_sc[r:P:QUADRANT, :].bitcast(I32),
             )

from contextlib import ExitStack

import concourse.mybir as mybir

K, T, J, R, L, N = 1024, 1024, 384, 512, 512, 512
FLOPS = 2 * J * (K * R + L * R + R * N)

F32 = mybir.dt.float32
BF16 = mybir.dt.bfloat16
I32 = mybir.dt.int32
U32 = mybir.dt.uint32
U16 = mybir.dt.uint16
U8 = mybir.dt.uint8
E4M3 = mybir.dt.float8_e4m3fn_x4
E5M2 = mybir.dt.float8_e5m2_x4
E2M1 = mybir.dt.float4_e2m1fn_x4
MULT, ADD, MAX = mybir.AluOpType.mult, mybir.AluOpType.add, mybir.AluOpType.max
COPY = mybir.ActivationFunctionType.Copy

P = 128
PACK = 4
PASSES = K // (P * PACK)
PLANES = PASSES * PACK
LAST = PLANES - 1
QUADRANT = 32
SCALE_ROWS = 4
LIST_COLUMN = 16
CH = 128
CHUNKS = J // CH
LEAD = 8
STEP = -0.6
LINE = 16
RUN = 4


def tile_list_steps_rival_residual_pl_kernel(
    tc, xf, fk, w_words, w_scales, sx_words, sx_scales, ws_words, ws_scales, wb_words, wb_scales, rs, gm, offs,
    out_0, out_1, out_2,
):
    nc = tc.nc
    with ExitStack() as ctx:
        sb = ctx.enter_context(tc.tile_pool(name="sb", bufs=1))
        ps = ctx.enter_context(tc.psum_pool(name="ps", bufs=1))

        def tile(name, shape, dtype, tag=None):
            return sb.tile(shape, dtype, name=name, tag=tag or name, align_bytes=64)

        offsets = sb.tile([P, J // LIST_COLUMN], U16, name="offsets")
        x = [tile("x%d" % k, [P, T], F32) for k in range(PLANES)]
        g_all = tile("g_all", [P, PLANES, LEAD + J], F32)
        g = [g_all[:, k, :] for k in range(PLANES)]
        zeros = tile("zeros", [P, PLANES], F32)
        d_all = tile("d_all", [P, PLANES, J], F32)
        d = [d_all[:, k, :] for k in range(PLANES)]
        fk_sb = tile("fk_sb", [P, PASSES, PACK], F32)
        gm_sb = tile("gm_sb", [P, PACK], F32)
        rs_sb = tile("rs_sb", [P, PACK, J], F32)

        w_raw = [tile("w_raw%d" % a, [P, R], U32) for a in range(PASSES)]
        w_dealt = tile("w_dealt", [P, PASSES, R], U32)
        w_sc_raw = tile("w_sc_raw", [P, PASSES, R], U8)
        w_sc = tile("w_sc", [P, PASSES, R], U8)
        ws_raw = tile("ws_raw", [P, 2 * R], U8)
        ws_dealt = tile("ws_dealt", [P, 2 * R], U8)
        ws_sc_raw = tile("ws_sc_raw", [P, R], U8)
        ws_sc = tile("ws_sc", [P, R], U8)
        sx_sb = tile("sx_sb", [P, 2 * J], U8)
        sx_sc = tile("sx_sc", [P, J], U8)
        wb_raw = tile("wb_raw", [P, N], U32)
        wb_dealt = tile("wb_dealt", [P, N], U32)
        wb_sc_raw = tile("wb_sc_raw", [P, N], U8)
        wb_sc = tile("wb_sc", [P, N], U8)

        x_planes = xf.rearrange("(a p t) c -> a t p c", a=PASSES, t=PACK)

        def load_x(k):
            nc.sync.dma_start(out=x[k][:], in_=x_planes[k // PACK, k % PACK])

        def load_words(dst, src):
            nc.sync.dma_start(out=dst[:].bitcast(I32), in_=src.rearrange("p n t -> p (n t)").bitcast(I32))

        def load_scales(dst, src, rows=range(SCALE_ROWS)):
            for r in rows:
                nc.sync.dma_start(
                    out=dst[r:P:QUADRANT].bitcast(I32),
                    in_=src.rearrange("z (s r) c -> r s z c", r=SCALE_ROWS)[r].bitcast(I32),
                )

        def one(t):
            return t[:].rearrange("p (z c) -> p z c", z=1)

        nc.gpsimd.memset(w_sc_raw[:].bitcast(I32), 0)
        nc.vector.memset(zeros[:], 0.0)
        nc.gpsimd.memset(ws_sc_raw[:].bitcast(I32), 0)
        nc.gpsimd.memset(wb_sc_raw[:].bitcast(I32), 0)
        nc.gpsimd.memset(sx_sc[:].bitcast(I32), 0)
        nc.scalar.activation(g_all[:, :, LEAD - 1], zeros[:], COPY)

        nc.sync.dma_start(out=fk_sb[:], in_=fk.rearrange("(a p t) o -> p a (t o)", a=PASSES, t=PACK))
        load_x(0)
        load_scales(w_sc_raw[:], w_scales)
        nc.sync.dma_start(offsets[:], offs)
        load_x(1)
        load_x(2)
        load_x(3)
        load_scales(one(ws_sc_raw), ws_scales)
        load_x(4)
        load_words(w_raw[0], w_words[0])
        load_scales(one(wb_sc_raw), wb_scales)
        load_scales(one(sx_sc), sx_scales, range(0, 1))
        load_x(5)
        load_x(6)
        load_scales(one(sx_sc), sx_scales, range(1, SCALE_ROWS))
        nc.sync.dma_start(out=ws_raw[:].bitcast(I32), in_=ws_words[0].bitcast(I32))
        nc.sync.dma_start(out=sx_sb[:].bitcast(I32), in_=sx_words[0].bitcast(I32))
        load_x(LAST)
        load_words(w_raw[1], w_words[1])
        load_words(wb_raw, wb_words[0])
        nc.sync.dma_start(out=gm_sb[:], in_=gm.rearrange("(p t) o -> p (t o)", t=PACK))
        nc.sync.dma_start(out=rs_sb[:], in_=rs.rearrange("(p t) j -> p t j", t=PACK))

        u_planes = tile("u_planes", [P, PLANES, J], BF16)
        u_bf = [tile("u_bf%d" % a, [P, J, PACK], BF16) for a in range(PASSES)]
        u_q = [tile("u_q%d" % a, [P, J], U32) for a in range(PASSES)]
        u_sc = [tile("u_sc%d" % a, [P, J], U8) for a in range(PASSES)]
        a_ps = [ps.tile([P, PACK, CH], F32, name="a_ps%d" % c) for c in range(CHUNKS)]

        def cols(c):
            return slice(c * CH, (c + 1) * CH)

        def gather(k, j0, j1):
            nc.scalar.activation(
                g[k][:, LEAD + j0 : LEAD + j1],
                x[k][:].indirect(offsets[:, j0 // LIST_COLUMN : j1 // LIST_COLUMN]),
                COPY,
            )

        def steps(out, src, j0, j1):
            nc.vector.scalar_tensor_tensor(
                out=out[:, j0:j1], in0=src[:, LEAD - 1 + j0 : LEAD - 1 + j1], scalar=STEP,
                in1=src[:, LEAD + j0 : LEAD + j1], op0=MULT, op1=ADD,
            )

        def fk_of(k):
            return fk_sb[:, k // PACK, k % PACK : k % PACK + 1]

        def make_u(k, j0, j1):
            steps(d[k], g[k], j0, j1)
            nc.vector.tensor_scalar(
                out=u_planes[:, k, j0:j1], in0=d[k][:, j0:j1], scalar1=fk_of(k), scalar2=None, op0=MULT
            )

        def weave(engine_copy, dst, src):
            engine_copy(
                out=dst.rearrange("p (c i) t -> p c t i", i=RUN), in_=src.rearrange("p t (c i) -> p c t i", i=RUN)
            )

        def quantize(q, sc, src):
            nc.vector.quantize_mx(out=q.bitcast(E4M3), scales=sc, in_=src.rearrange("p j t -> p (j t)"))

        def deal(engine_copy, dst, src, item_bytes):
            run = LINE // item_bytes
            engine_copy(
                out=dst.rearrange("p z (t c i) -> p z c t i", t=PACK, i=run),
                in_=src.rearrange("p z (c i t) -> p z c t i", t=PACK, i=run),
            )

        def first_product(a, c):
            for t in range(PACK):
                m = slice(t * P, (t + 1) * P)
                nc.tensor.matmul_mx(
                    out=a_ps[c][:, t, :], lhsT=w_dealt[:, a, m].bitcast(E5M2), lhsT_scale=w_sc[:, a, m],
                    rhs=u_q[a][:, cols(c)].bitcast(E4M3), rhs_scale=u_sc[a][:, cols(c)],
                    start=(a == 0 and t == 0), stop=(a == PASSES - 1 and t == PACK - 1),
                )

        def rival_product(c):
            b_ps = ps.tile([P, PACK, CH], F32, name="b_ps%d" % c, tag="bank%d" % c)
            for t in range(PACK):
                nc.tensor.matmul_mx(
                    out=b_ps[:, t, :], lhsT=ws_dealt[:, 2 * t * P : 2 * (t + 1) * P].bitcast(E2M1),
                    lhsT_scale=ws_sc[:, t * P : (t + 1) * P],
                    rhs=sx_sb[:, 2 * c * CH : 2 * (c + 1) * CH].bitcast(E2M1), rhs_scale=sx_sc[:, cols(c)],
                    start=True, stop=True,
                )
            return b_ps

        deal(nc.vector.tensor_copy, w_sc[:], w_sc_raw[:], 1)
        for k in range(PACK):
            gather(k, 0, J)
            make_u(k, 0, J)
        weave(nc.vector.tensor_copy, u_bf[0][:], u_planes[:, 0:PACK, :])
        deal(nc.vector.tensor_copy, one(ws_sc), one(ws_sc_raw), 1)
        quantize(u_q[0][:], u_sc[0][:], u_bf[0][:])

        gather(PACK, 0, J)
        make_u(PACK, 0, J)
        deal(nc.scalar.copy, w_dealt[:, 0:1, :], one(w_raw[0]), 4)
        deal(nc.vector.tensor_copy, one(wb_sc), one(wb_sc_raw), 1)
        for c in range(CHUNKS):
            first_product(0, c)
        for k in range(PACK + 1, LAST):
            gather(k, 0, J)
            make_u(k, 0, J)
        deal(nc.scalar.copy, one(ws_dealt).bitcast(U16), one(ws_raw).bitcast(U16), 2)

        for c in range(CHUNKS):
            gather(LAST, c * CH, (c + 1) * CH)
        deal(nc.scalar.copy, w_dealt[:, 1:2, :], one(w_raw[1]), 4)
        b2 = tile("b2", [P, CHUNKS, CH, PACK], F32, tag="w_raw1")
        for c in range(CHUNKS):
            nc.scalar.copy(out=b2[:, c], in_=rival_product(c)[:].rearrange("p t j -> p j t"))
        for c in range(CHUNKS):
            make_u(LAST, c * CH, (c + 1) * CH)
            weave(nc.vector.tensor_copy, u_bf[1][:, cols(c), :], u_planes[:, PACK:, cols(c)])
            quantize(u_q[1][:, cols(c)], u_sc[1][:, cols(c)], u_bf[1][:, cols(c), :])
            first_product(1, c)
        deal(nc.scalar.copy, one(wb_dealt), one(wb_raw), 4)

        hid = [tile("hid%d" % c, [P, CH, PACK], BF16) for c in range(CHUNKS)]
        h_q = tile("h_q", [P, J], U32)
        h_sc = tile("h_sc", [P, J], U8)
        y = [tile("y%d" % c, [P, PACK, CH], F32) for c in range(CHUNKS)]
        y_bf = [tile("y_bf%d" % c, [P, CH, PACK], BF16) for c in range(CHUNKS)]
        y_q = tile("y_q", [P, J], U32)
        y_sc = tile("y_sc", [P, J], U8)
        p_ps = []
        for c in range(CHUNKS):
            nc.vector.tensor_tensor(
                out=hid[c][:], in0=a_ps[c][:].rearrange("p t j -> p j t"), in1=b2[:, c], op=MAX
            )
            quantize(h_q[:, cols(c)], h_sc[:, cols(c)], hid[c][:])
            p_ps.append(ps.tile([P, PACK, CH], F32, name="p_ps%d" % c, tag="bank%d" % c))
            for t in range(PACK):
                m = slice(t * P, (t + 1) * P)
                nc.tensor.matmul_mx(
                    out=p_ps[c][:, t, :], lhsT=wb_dealt[:, m].bitcast(E5M2), lhsT_scale=wb_sc[:, m],
                    rhs=h_q[:, cols(c)].bitcast(E4M3), rhs_scale=h_sc[:, cols(c)], start=True, stop=True,
                )

        out_y = out_0.rearrange("(p t) j -> p t j", t=PACK)
        out_words = out_1[0].rearrange("p j t -> p (j t)").bitcast(I32)
        for c in range(CHUNKS):
            for t in range(PACK):
                nc.vector.scalar_tensor_tensor(
                    out=y[c][:, t, :], in0=p_ps[c][:, t, :], scalar=gm_sb[:, t : t + 1], in1=rs_sb[:, t, cols(c)],
                    op0=MULT, op1=ADD,
                )
            nc.sync.dma_start(out=out_y[:, :, cols(c)], in_=y[c][:])
            weave(nc.scalar.copy if c < CHUNKS - 1 else nc.vector.tensor_copy, y_bf[c][:], y[c][:])
        for c in range(CHUNKS):
            quantize(y_q[:, cols(c)], y_sc[:, cols(c)], y_bf[c][:])
        early = (CHUNKS - 1) * CH
        nc.sync.dma_start(out=out_words[:, :early], in_=y_q[:, :early].bitcast(I32))
        nc.sync.dma_start(out=out_words[:, early:], in_=y_q[:, early:].bitcast(I32))
        for r in range(SCALE_ROWS):
            queue = nc.sync if r % 2 else nc.scalar
            queue.dma_start(
                out=out_2[0].rearrange("(s r) c -> r s c", r=SCALE_ROWS)[r].bitcast(I32),
                in_=y_sc[r:P:QUADRANT, :].bitcast(I32),
            )
